import numpy as np
import ml_dtypes

BF16 = ml_dtypes.bfloat16


def bf(x):
    return np.asarray(x, np.float32).astype(BF16)


def f32(x):
    return np.asarray(x, np.float32)


def f64(x):
    return np.asarray(x).astype(np.float64)


def striped(idx):
    return np.tile(idx.reshape(-1, 16).T, (8, 1))


def rows(idx, k):
    return np.tile(idx, (k, 1))


def look(tab, idx):
    return np.take_along_axis(f64(tab), rows(idx, len(tab)), axis=1)


K, S, V, N, M = 256, 2048, 512, 512, 128


def setup_inputs():
    return {"tab": f32(np.random.standard_normal((2, K, S))), "y": f32(np.random.standard_normal((K, V))), "w": bf(np.random.standard_normal((K, M)) / np.sqrt(K)), "b": f32(0.5 * np.random.standard_normal((M, 1))), "offs": striped(np.random.permutation(S)[:N])}


def reference(tab, y, w, b, offs):
    idx = offs[:16].T.reshape(-1)
    x = (look(tab[0], idx) - f64(y)) * (1.0 / (1.0 + np.exp(-look(tab[1], idx))))
    return np.maximum(f64(w).T @ x + f64(b), 0.0)

@@ -1,0 +1,45 @@
+import concourse.mybir as mybir
+
+P = 128
+FLOPS = 2 * 256 * 128 * 512
+
+F32, BF16, U16 = mybir.dt.float32, mybir.dt.bfloat16, mybir.dt.uint16
+ALU = mybir.AluOpType
+ACT = mybir.ActivationFunctionType
+
+
+def tile_lookup_vg_subsig_relu_kernel(tc, tab, y, w, b, offs, out):
+    nc = tc.nc
+    rows, places = tab.shape[1], tab.shape[2]
+    n, m = y.shape[1], w.shape[1]
+    blocks = rows // P
+    with (
+        tc.tile_pool(name="held", bufs=1) as held,
+        tc.psum_pool(name="psum", bufs=1) as psum,
+    ):
+        offsets = held.tile([P, n // 16], U16, name="offsets")
+        nc.sync.dma_start(offsets[:], offs)
+        bias = held.tile([m, 1], F32, name="bias")
+        nc.gpsimd.dma_start(bias[:], b)
+        product = psum.tile([m, n], F32, name="product")
+        for k in range(blocks):
+            block = slice(k * P, (k + 1) * P)
+            stream = held.tile([P, n], F32, name=f"stream{k}")
+            weights = held.tile([P, m], BF16, name=f"weights{k}")
+            values = held.tile([P, places], F32, name=f"values{k}")
+            gates = held.tile([P, places], F32, name=f"gates{k}")
+            nc.gpsimd.dma_start(weights[:], w[block, :])
+            nc.sync.dma_start(stream[:], y[block, :])
+            nc.sync.dma_start(values[:], tab[0, block, :])
+            nc.sync.dma_start(gates[:], tab[1, block, :])
+
+            diff = held.tile([P, n], F32, name=f"diff{k}")
+            gate = held.tile([P, n], F32, name=f"gate{k}")
+            x = held.tile([P, n], BF16, name=f"x{k}")
+            nc.vector.tensor_tensor(diff[:], values[:].indirect(offsets[:]), stream[:], ALU.subtract)
+            nc.scalar.activation(gate[:], gates[:].indirect(offsets[:]), ACT.Sigmoid)
+            nc.vector.tensor_tensor(x[:], diff[:], gate[:], ALU.mult)
+            nc.tensor.matmul(product[:], weights[:], x[:], start=(k == 0), stop=(k == blocks - 1))
+        result = held.tile([m, n], F32, name="result")
+        nc.scalar.activation(result[:], product[:], ACT.Relu, bias=bias[:])
+        nc.sync.dma_start(out, result[:])

@@ -1,6 +1,7 @@
 import concourse.mybir as mybir
 
 P = 128
+PIECES = 4
 FLOPS = 2 * 256 * 128 * 512
 
 F32, BF16, U16 = mybir.dt.float32, mybir.dt.bfloat16, mybir.dt.uint16
@@ -13,33 +14,50 @@ def tile_lookup_vg_subsig_relu_kernel(tc, tab, y, w, b, offs, out):
     rows, places = tab.shape[1], tab.shape[2]
     n, m = y.shape[1], w.shape[1]
     blocks = rows // P
+    width = n // PIECES
+    tab_blocks = tab.rearrange("t (p k) s -> t k p s", k=blocks)
     with (
         tc.tile_pool(name="held", bufs=1) as held,
         tc.psum_pool(name="psum", bufs=1) as psum,
     ):
+        values = [held.tile([P, places], F32, name=f"values{k}") for k in range(blocks)]
+        gates = [held.tile([P, places], F32, name=f"gates{k}") for k in range(blocks)]
         offsets = held.tile([P, n // 16], U16, name="offsets")
-        nc.sync.dma_start(offsets[:], offs)
+        stream = held.tile([P, blocks * n], F32, name="stream")
+        weights = held.tile([P, blocks * m], BF16, name="weights")
         bias = held.tile([m, 1], F32, name="bias")
-        nc.gpsimd.dma_start(bias[:], b)
-        product = psum.tile([m, n], F32, name="product")
-        for k in range(blocks):
-            block = slice(k * P, (k + 1) * P)
-            stream = held.tile([P, n], F32, name=f"stream{k}")
-            weights = held.tile([P, m], BF16, name=f"weights{k}")
-            values = held.tile([P, places], F32, name=f"values{k}")
-            gates = held.tile([P, places], F32, name=f"gates{k}")
-            nc.gpsimd.dma_start(weights[:], w[block, :])
-            nc.sync.dma_start(stream[:], y[block, :])
-            nc.sync.dma_start(values[:], tab[0, block, :])
-            nc.sync.dma_start(gates[:], tab[1, block, :])
 
+        nc.sync.dma_start(gates[0][:], tab_blocks[1, 0])
+        nc.sync.dma_start(offsets[:], offs)
+        nc.sync.dma_start(values[0][:], tab_blocks[0, 0])
+        nc.sync.dma_start(stream[:], y.rearrange("(p k) n -> p (k n)", k=blocks))
+        nc.scalar.dma_start(weights[:], w.rearrange("(p k) m -> p (k m)", k=blocks))
+        nc.scalar.dma_start(bias[:], b)
+        for k in range(1, blocks):
+            nc.sync.dma_start(values[k][:], tab_blocks[0, k])
+            nc.sync.dma_start(gates[k][:], tab_blocks[1, k])
+
+        products = [psum.tile([m, width], F32, name=f"product{i}") for i in range(PIECES)]
+        for k in range(blocks):
             diff = held.tile([P, n], F32, name=f"diff{k}")
             gate = held.tile([P, n], F32, name=f"gate{k}")
             x = held.tile([P, n], BF16, name=f"x{k}")
-            nc.vector.tensor_tensor(diff[:], values[:].indirect(offsets[:]), stream[:], ALU.subtract)
-            nc.scalar.activation(gate[:], gates[:].indirect(offsets[:]), ACT.Sigmoid)
-            nc.vector.tensor_tensor(x[:], diff[:], gate[:], ALU.mult)
-            nc.tensor.matmul(product[:], weights[:], x[:], start=(k == 0), stop=(k == blocks - 1))
+            nc.vector.tensor_tensor(
+                diff[:], values[k][:].indirect(offsets[:]), stream[:, k * n : (k + 1) * n], ALU.subtract
+            )
+            for i in range(PIECES):
+                piece = slice(i * width, (i + 1) * width)
+                piece_offsets = offsets[:, i * width // 16 : (i + 1) * width // 16]
+                nc.scalar.activation(gate[:, piece], gates[k][:].indirect(piece_offsets), ACT.Sigmoid)
+            for i in range(PIECES):
+                piece = slice(i * width, (i + 1) * width)
+                nc.vector.tensor_tensor(x[:, piece], diff[:, piece], gate[:, piece], ALU.mult)
+                nc.tensor.matmul(
+                    products[i][:], weights[:, k * m : (k + 1) * m], x[:, piece],
+                    start=(k == 0), stop=(k == blocks - 1),
+                )
         result = held.tile([m, n], F32, name="result")
-        nc.scalar.activation(result[:], product[:], ACT.Relu, bias=bias[:])
-        nc.sync.dma_start(out, result[:])
+        for i in range(PIECES):
+            piece = slice(i * width, (i + 1) * width)
+            nc.scalar.activation(result[:, piece], products[i][:], ACT.Relu, bias=bias[:])
+            nc.sync.dma_start(out[:, piece], result[:, piece])

@@ -1,7 +1,6 @@
 import concourse.mybir as mybir
 
 P = 128
-PIECES = 4
 FLOPS = 2 * 256 * 128 * 512
 
 F32, BF16, U16 = mybir.dt.float32, mybir.dt.bfloat16, mybir.dt.uint16
@@ -14,8 +13,11 @@ def tile_lookup_vg_subsig_relu_kernel(tc, tab, y, w, b, offs, out):
     rows, places = tab.shape[1], tab.shape[2]
     n, m = y.shape[1], w.shape[1]
     blocks = rows // P
-    width = n // PIECES
+    halves = [slice(0, 3 * n // 4), slice(3 * n // 4, n)]
+    pieces = [slice(i * n // 4, (i + 1) * n // 4) for i in range(4)]
+    early = blocks * n - n // 4
     tab_blocks = tab.rearrange("t (p k) s -> t k p s", k=blocks)
+    y_rows = y.rearrange("(p k) n -> p (k n)", k=blocks)
     with (
         tc.tile_pool(name="held", bufs=1) as held,
         tc.psum_pool(name="psum", bufs=1) as psum,
@@ -27,37 +29,39 @@ def tile_lookup_vg_subsig_relu_kernel(tc, tab, y, w, b, offs, out):
         weights = held.tile([P, blocks * m], BF16, name="weights")
         bias = held.tile([m, 1], F32, name="bias")
 
+        def listed(window, cols):
+            return window[:].indirect(offsets[:, cols.start // 16 : cols.stop // 16])
+
         nc.sync.dma_start(gates[0][:], tab_blocks[1, 0])
         nc.sync.dma_start(offsets[:], offs)
         nc.sync.dma_start(values[0][:], tab_blocks[0, 0])
-        nc.sync.dma_start(stream[:], y.rearrange("(p k) n -> p (k n)", k=blocks))
-        nc.scalar.dma_start(weights[:], w.rearrange("(p k) m -> p (k m)", k=blocks))
-        nc.scalar.dma_start(bias[:], b)
+        nc.sync.dma_start(stream[:, :early], y_rows[:, :early])
         for k in range(1, blocks):
             nc.sync.dma_start(values[k][:], tab_blocks[0, k])
             nc.sync.dma_start(gates[k][:], tab_blocks[1, k])
+        nc.sync.dma_start(stream[:, early:], y_rows[:, early:])
+        nc.sync.dma_start(weights[:], w.rearrange("(p k) m -> p (k m)", k=blocks))
+        nc.sync.dma_start(bias[:], b)
 
-        products = [psum.tile([m, width], F32, name=f"product{i}") for i in range(PIECES)]
+        products = [
+            psum.tile([m, piece.stop - piece.start], F32, name=f"product{i}") for i, piece in enumerate(pieces)
+        ]
         for k in range(blocks):
             diff = held.tile([P, n], F32, name=f"diff{k}")
             gate = held.tile([P, n], F32, name=f"gate{k}")
             x = held.tile([P, n], BF16, name=f"x{k}")
-            nc.vector.tensor_tensor(
-                diff[:], values[k][:].indirect(offsets[:]), stream[:, k * n : (k + 1) * n], ALU.subtract
-            )
-            for i in range(PIECES):
-                piece = slice(i * width, (i + 1) * width)
-                piece_offsets = offsets[:, i * width // 16 : (i + 1) * width // 16]
-                nc.scalar.activation(gate[:, piece], gates[k][:].indirect(piece_offsets), ACT.Sigmoid)
-            for i in range(PIECES):
-                piece = slice(i * width, (i + 1) * width)
+            stream_k = stream[:, k * n : (k + 1) * n]
+            for half in halves:
+                nc.vector.tensor_tensor(diff[:, half], listed(values[k], half), stream_k[:, half], ALU.subtract)
+            for piece in pieces:
+                nc.scalar.activation(gate[:, piece], listed(gates[k], piece), ACT.Sigmoid)
+            for piece, product in zip(pieces, products):
                 nc.vector.tensor_tensor(x[:, piece], diff[:, piece], gate[:, piece], ALU.mult)
                 nc.tensor.matmul(
-                    products[i][:], weights[:, k * m : (k + 1) * m], x[:, piece],
+                    product[:], weights[:, k * m : (k + 1) * m], x[:, piece],
                     start=(k == 0), stop=(k == blocks - 1),
                 )
         result = held.tile([m, n], F32, name="result")
-        for i in range(PIECES):
-            piece = slice(i * width, (i + 1) * width)
-            nc.scalar.activation(result[:, piece], products[i][:], ACT.Relu, bias=bias[:])
+        for piece, product in zip(pieces, products):
+            nc.scalar.activation(result[:, piece], product[:], ACT.Relu, bias=bias[:])
             nc.sync.dma_start(out[:, piece], result[:, piece])

import concourse.mybir as mybir

P = 128
FLOPS = 2 * 256 * 128 * 512

F32, BF16, U16 = mybir.dt.float32, mybir.dt.bfloat16, mybir.dt.uint16
ALU = mybir.AluOpType
ACT = mybir.ActivationFunctionType


def tile_lookup_vg_subsig_relu_kernel(tc, tab, y, w, b, offs, out):
    nc = tc.nc
    rows, places = tab.shape[1], tab.shape[2]
    n, m = y.shape[1], w.shape[1]
    blocks = rows // P
    halves = [slice(0, 3 * n // 4), slice(3 * n // 4, n)]
    pieces = [slice(i * n // 4, (i + 1) * n // 4) for i in range(4)]
    early = blocks * n - n // 4
    tab_blocks = tab.rearrange("t (p k) s -> t k p s", k=blocks)
    y_rows = y.rearrange("(p k) n -> p (k n)", k=blocks)
    with (
        tc.tile_pool(name="held", bufs=1) as held,
        tc.psum_pool(name="psum", bufs=1) as psum,
    ):
        values = [held.tile([P, places], F32, name=f"values{k}") for k in range(blocks)]
        gates = [held.tile([P, places], F32, name=f"gates{k}") for k in range(blocks)]
        offsets = held.tile([P, n // 16], U16, name="offsets")
        stream = held.tile([P, blocks * n], F32, name="stream")
        weights = held.tile([P, blocks * m], BF16, name="weights")
        bias = held.tile([m, 1], F32, name="bias")

        def listed(window, cols):
            return window[:].indirect(offsets[:, cols.start // 16 : cols.stop // 16])

        nc.sync.dma_start(gates[0][:], tab_blocks[1, 0])
        nc.sync.dma_start(offsets[:], offs)
        nc.sync.dma_start(values[0][:], tab_blocks[0, 0])
        nc.sync.dma_start(stream[:, :early], y_rows[:, :early])
        for k in range(1, blocks):
            nc.sync.dma_start(values[k][:], tab_blocks[0, k])
            nc.sync.dma_start(gates[k][:], tab_blocks[1, k])
        nc.sync.dma_start(stream[:, early:], y_rows[:, early:])
        nc.sync.dma_start(weights[:], w.rearrange("(p k) m -> p (k m)", k=blocks))
        nc.sync.dma_start(bias[:], b)

        products = [
            psum.tile([m, piece.stop - piece.start], F32, name=f"product{i}") for i, piece in enumerate(pieces)
        ]
        for k in range(blocks):
            diff = held.tile([P, n], F32, name=f"diff{k}")
            gate = held.tile([P, n], F32, name=f"gate{k}")
            x = held.tile([P, n], BF16, name=f"x{k}")
            stream_k = stream[:, k * n : (k + 1) * n]
            for half in halves:
                nc.vector.tensor_tensor(diff[:, half], listed(values[k], half), stream_k[:, half], ALU.subtract)
            for piece in pieces:
                nc.scalar.activation(gate[:, piece], listed(gates[k], piece), ACT.Sigmoid)
            for piece, product in zip(pieces, products):
                nc.vector.tensor_tensor(x[:, piece], diff[:, piece], gate[:, piece], ALU.mult)
                nc.tensor.matmul(
                    product[:], weights[:, k * m : (k + 1) * m], x[:, piece],
                    start=(k == 0), stop=(k == blocks - 1),
                )
        result = held.tile([m, n], F32, name="result")
        for piece, product in zip(pieces, products):
            nc.scalar.activation(result[:, piece], product[:], ACT.Relu, bias=bias[:])
            nc.sync.dma_start(out[:, piece], result[:, piece])
